import numpy as np
import ml_dtypes


def mxq(x, axis, fmt="e4m3"):
    dtype, down = {"e4m3": (ml_dtypes.float8_e4m3fn, 7), "e5m2": (ml_dtypes.float8_e5m2, 14)}[fmt]
    v = np.moveaxis(np.asarray(x, np.float32).astype(ml_dtypes.bfloat16).astype(np.float64), axis, -1)
    blocks = v.reshape(v.shape[:-1] + (-1, 32))
    amax = np.abs(blocks).max(-1, keepdims=True)
    byte = np.maximum(np.where(amax > 0, np.frexp(amax)[1] - 1 + 127, 0) - down, 1)
    scale = np.exp2(byte - 127.0)
    codes = (blocks / scale).astype(np.float32).astype(dtype).astype(np.float64)
    return np.moveaxis((codes * scale).reshape(v.shape), -1, axis)


WIDE = False


def mx_kscale(k):
    if not WIDE:
        return np.ones(k)
    levels = np.array([10, -10, 5, -5, 0])
    if k % 512:
        return np.exp2(np.random.permutation(np.resize(levels, k // 32))).repeat(32)
    a = np.empty((k // 512, 16))
    for p in range(k // 512):
        a[p, :8] = np.random.permutation(np.resize(levels, 8))
        for g in range(8):
            far = levels[np.abs(levels - a[p, g]) >= 10]
            a[p, g + 8] = far[np.random.randint(len(far))]
    return np.exp2(a.ravel()).repeat(32)


BF16 = ml_dtypes.bfloat16


def bf(x):
    return np.asarray(x, np.float32).astype(BF16)


def f64(x):
    return np.asarray(x).astype(np.float64)


E2M1 = np.array([0.0, 0.5, 1.0, 1.5, 2.0, 3.0, 4.0, 6.0, -0.0, -0.5, -1.0, -1.5, -2.0, -3.0, -4.0, -6.0])


def pack_weight(w, fmt):
    k, n = w.shape
    w = f64(bf(w)).reshape(k // 32, 32, n)
    amax = np.abs(w).max(1)
    if fmt == "e4m3":
        byte = np.frexp(amax)[1] - 1 + 127 - 7
    else:
        mant, ex = np.frexp(amax / 6.0)
        byte = np.where(mant > 0.5, ex, ex - 1) + 127
    byte = np.clip(np.where(amax > 0, byte, 1), 1, 254)
    scaled = (w * np.exp2(127.0 - byte)[:, None, :]).reshape(k, n).astype(np.float32)
    by_word = np.ascontiguousarray(scaled.reshape(k // 512, 128, 4, n).transpose(0, 1, 3, 2))
    if fmt == "e4m3":
        words = by_word.astype(ml_dtypes.float8_e4m3fn).view(np.uint8)
    else:
        c = by_word.astype(ml_dtypes.float4_e2m1fn).view(np.uint8) & 0xF
        words = c[..., 0::2] | (c[..., 1::2] << 4)
    return np.ascontiguousarray(words), np.ascontiguousarray(byte.astype(np.uint8).reshape(k // 512, 16, n))


def unpack_weight(words, scales, fmt):
    g, p, n, _ = words.shape
    if fmt == "e4m3":
        vals = np.ascontiguousarray(words).view(ml_dtypes.float8_e4m3fn).astype(np.float64)
    else:
        nib = np.empty((g, p, n, 4), np.uint8)
        nib[..., 0::2] = words & 0xF
        nib[..., 1::2] = words >> 4
        vals = E2M1[nib]
    vals = vals * np.repeat(np.exp2(scales.astype(np.float64) - 127.0), 8, axis=1)[..., None]
    return vals.transpose(0, 1, 3, 2).reshape(g * 512, n)

E4M3FN = np.array([(-1.0 if i & 128 else 1.0) * ((1.0 + (i & 7) / 8.0) * 2.0 ** (((i >> 3) & 15) - 7) if i & 120 else (i & 7) * 2.0 ** -9) for i in range(256)])


def e4m3fn_bytes(y):
    return np.clip(np.asarray(y, np.float64), -448.0, 448.0).astype(np.float32).astype(ml_dtypes.float8_e4m3fn).view(np.uint8)


def e4m3fn_values(b):
    return E4M3FN[b]


Q, K, D, F = 1024, 1024, 512, 1024


def draw0():
    s, t = mx_kscale(D), mx_kscale(F)
    x = bf(np.random.standard_normal((Q, D)) * s)
    y = bf(np.random.standard_normal((K, D)) * s)
    words, scales = pack_weight(np.random.standard_normal((D, F)) / np.sqrt(D) / s[:, None], "e4m3")
    return {"x": x,
            "y": y,
            "w_words": words,
            "w_scales": scales,
            "role": bf(np.random.uniform(-np.pi, np.pi, F)),
            "a": bf((1.0 + 0.1 * np.random.standard_normal(F)) * t),
            "c": bf((1.0 + 0.1 * np.random.standard_normal(F)) / t)}


def phasor_parts(amplitude, phase):
    return amplitude[None, :] * np.cos(phase), amplitude[None, :] * np.sin(phase)


def core(x, y, w_words, w_scales, role, a, c):
    wq = unpack_weight(w_words, w_scales, "e4m3")
    f = wq.shape[1]
    theta = mxq(f64(x), 1, "e4m3") @ wq
    phi = (mxq(f64(y), 1, "e4m3") @ wq) + f64(role)[None, :]
    qre, qim = phasor_parts(f64(a), theta)
    kre, kim = phasor_parts(f64(c), phi)
    re = mxq(qre, 1, "e4m3") @ mxq(kre, 1, "e4m3").T
    im = mxq(qim, 1, "e4m3") @ mxq(kim, 1, "e4m3").T
    return (re + im) / np.sqrt(f)


def setup_inputs():
    drawn = draw0()
    full = np.asarray(drawn['y']).astype(np.float64)
    scale = (np.abs(full).reshape(1024, 4, 128).max(axis=(2,)) / 448.0).astype(np.float32)
    given = {}
    for key, value in drawn.items():
        if key == 'y':
            given['y_bytes'] = e4m3fn_bytes(full / np.repeat(scale.astype(np.float64), 128, axis=1))
            given['y_scale'] = scale
        else:
            given[key] = value
    return given


def reference(x, y_bytes, y_scale, w_words, w_scales, role, a, c):
    return core(x, e4m3fn_values(y_bytes) * np.repeat(y_scale.astype(np.float64), 128, axis=1), w_words, w_scales, role, a, c)

@@ -1,0 +1,276 @@
+import math
+from contextlib import ExitStack
+
+import concourse.mybir as mybir
+from concourse.masks import make_identity
+
+F32 = mybir.dt.float32
+BF16 = mybir.dt.bfloat16
+I32 = mybir.dt.int32
+U32 = mybir.dt.uint32
+U8 = mybir.dt.uint8
+FP8 = mybir.dt.float8_e4m3fn
+FP8X4 = mybir.dt.float8_e4m3fn_x4
+ALU = mybir.AluOpType
+ACTF = mybir.ActivationFunctionType
+
+P = 128
+TOK = 1024
+D = 512
+FREQ = 1024
+HALF = 512
+PI = math.pi
+FLOPS = 2 * 2 * TOK * D * FREQ + 2 * 2 * TOK * TOK * FREQ
+
+
+def tile_fhrrbounditemsimilarity_d1p_kernel(tc, x, y_bytes, y_scale, w_words, w_scales, role, a, c, out):
+    nc = tc.nc
+    with ExitStack() as ctx:
+        keep = ctx.enter_context(tc.tile_pool(name="keep", bufs=1))
+        work = ctx.enter_context(tc.tile_pool(name="work", bufs=2))
+        psum = ctx.enter_context(tc.psum_pool(name="psum", bufs=4))
+        ctx.enter_context(tc.manual_schedule())
+
+        ident = keep.tile([P, P], F32, name="ident")
+        make_identity(nc, ident[:])
+        zero = keep.tile([P, 1], F32, name="zero")
+        nc.vector.memset(zero[:], 0.0)
+        wsraw = keep.tile([P, FREQ], U8, name="wsraw", align_bytes=64)
+        nc.vector.memset(wsraw[:].bitcast(I32), 0)
+
+        ysc = keep.tile([P, 8, 4], F32, name="ysc")
+        nc.scalar.dma_start(out=ysc[:], in_=y_scale.rearrange("(i p) j -> p i j", p=P))
+        vec = {}
+        for name, v in (("role", role), ("a", a), ("c", c)):
+            t = keep.tile([P, 2, 4], BF16, name=f"vec_{name}")
+            nc.scalar.dma_start(out=t[:], in_=v.rearrange("(g p t) -> p g t", g=2, t=4))
+            vec[name] = t
+
+        x_sb = []
+        y_sb = []
+        xv = x.rearrange("(h i p) k -> h p i k", p=P, i=4)
+        yv = y_bytes.rearrange("(h i p) k -> h p i k", p=P, i=4)
+        for h in range(2):
+            xt = keep.tile([P, 4, D], BF16, name=f"x_sb{h}", align_bytes=64)
+            yt = keep.tile([P, 4, D], U8, name=f"y_sb{h}", align_bytes=64)
+            x_sb.append(xt)
+            y_sb.append(yt)
+        wraw = keep.tile([P, FREQ], U32, name="wraw", align_bytes=64)
+        for b in range(2):
+            nc.sync.dma_start(out=x_sb[0][:, 2 * b : 2 * b + 2, :], in_=xv[0][:, 2 * b : 2 * b + 2, :])
+        for q in range(4):
+            nc.sync.dma_start(out=wsraw[32 * q : 32 * q + 4, :].bitcast(I32), in_=w_scales[0, 4 * q : 4 * q + 4, :].bitcast(I32))
+        nc.sync.dma_start(out=wraw[:].bitcast(I32), in_=w_words[0].rearrange("p n t -> p (n t)").bitcast(I32))
+        nc.sync.dma_start(out=y_sb[0][:], in_=yv[0])
+        nc.sync.dma_start(out=x_sb[1][:], in_=xv[1])
+        nc.sync.dma_start(out=y_sb[1][:], in_=yv[1])
+
+        half_pi = keep.tile([P, 1], F32, name="half_pi")
+        nc.vector.tensor_scalar(half_pi[:], zero[:], PI / 2, None, op0=ALU.add)
+        warm = keep.tile([P, 1], F32, name="warm")
+        nc.scalar.activation(out=warm[:], in_=zero[:], func=ACTF.Sin)
+        role_k = keep.tile([P, 2, 4], F32, name="role_k")
+        role_s = keep.tile([P, 2, 4], F32, name="role_s")
+        role_c = keep.tile([P, 2, 4], F32, name="role_c")
+        a32 = keep.tile([P, 2, 4], F32, name="a32")
+
+        wp = keep.tile([P, FREQ], U32, name="wp", align_bytes=64)
+        wsp = keep.tile([P, FREQ], U8, name="wsp", align_bytes=64)
+
+        def weights():
+            nc.vector.tensor_copy(
+                out=wp[:].bitcast(I32).rearrange("p (g t m) -> p g t m", g=2, t=4),
+                in_=wraw[:].bitcast(I32).rearrange("p (g m t) -> p g t m", g=2, t=4),
+            )
+            nc.vector.tensor_copy(
+                out=wsp[:].rearrange("p (g t m) -> p g t m", g=2, t=4),
+                in_=wsraw[:].rearrange("p (g m t) -> p g t m", g=2, t=4),
+            )
+
+        def constants():
+            nc.vector.tensor_scalar(role_k[:], vec["role"][:], -PI / 4, None, op0=ALU.add)
+            nc.vector.tensor_copy(out=role_c[:], in_=vec["role"][:])
+            nc.vector.tensor_scalar(role_s[:], vec["role"][:], -PI / 2, None, op0=ALU.add)
+            nc.vector.tensor_copy(out=a32[:], in_=vec["a"][:])
+
+        codes = {}
+
+        def turn(side, h, src, engines):
+            words = src[:].bitcast(F32)
+            grouped = work.tile([P, HALF, 4], BF16, name="grouped", align_bytes=64)
+            flat = grouped[:].rearrange("p n t -> p (n t)")
+            gw = flat.bitcast(F32).rearrange("p (i r u) -> p i r u", i=4, u=2)
+            for b in range(2):
+                tp = psum.tile([P, 2, 2, P], F32, name="tp", tag="ps")
+                for i in range(2):
+                    for u in range(2):
+                        nc.tensor.transpose(tp[:, i, u, :], words[:, 2 * b + i, u : D // 2 : 2], ident[:])
+                engines[b](out=gw[:, 2 * b : 2 * b + 2], in_=tp[:].rearrange("p i u r -> p i r u"))
+            cd = keep.tile([P, HALF], U32, name=f"in_codes_{side}{h}", align_bytes=64)
+            sc = keep.tile([P, HALF], U8, name=f"in_scales_{side}{h}", align_bytes=64)
+            nc.vector.quantize_mx(out=cd[:].bitcast(FP8X4), scales=sc[:], in_=flat)
+            codes[side, h] = (cd, sc)
+
+        def widen(h):
+            yb = work.tile([P, 4, D], BF16, name="y_bf", align_bytes=64)
+            for i in range(4):
+                for j in range(4):
+                    cols = slice(128 * j, 128 * j + 128)
+                    nc.scalar.activation(
+                        out=yb[:, i, cols], in_=y_sb[h][:, i, cols].bitcast(FP8), func=ACTF.Copy, scale=ysc[:, 4 * h + i, j : j + 1]
+                    )
+            return yb
+
+        phasor = {}
+        state = {}
+
+        def matmuls(ch):
+            side, h, g = ch
+            cd, sc = codes[side, h]
+            banks = []
+            for t in range(4):
+                ps = psum.tile([P, HALF], F32, name="ps", tag="ps")
+                col = slice((4 * g + t) * P, (4 * g + t + 1) * P)
+                nc.tensor.matmul_mx(
+                    out=ps[:], lhsT=wp[:, col].bitcast(FP8X4), lhsT_scale=wsp[:, col],
+                    rhs=cd[:].bitcast(FP8X4), rhs_scale=sc[:], start=True, stop=True,
+                )
+                banks.append(ps)
+            state[ch, "banks"] = banks
+
+        def reduce(ch):
+            side, h, g = ch
+            banks = state[ch, "banks"]
+            k_sb = work.tile([P, 4, HALF], I32, name="k_sb", align_bytes=64)
+            r_sb = work.tile([P, 4, HALF], F32, name="r_sb", align_bytes=64)
+            period = PI if side == "q" else 2 * PI
+
+            def count(t):
+                off = PI / 4 if side == "q" else role_k[:, g, t : t + 1]
+                nc.vector.tensor_scalar(k_sb[:, t, :], banks[t][:], off, 1.0 / period, op0=ALU.add, op1=ALU.mult)
+
+            def rest(t):
+                nc.vector.scalar_tensor_tensor(
+                    out=r_sb[:, t, :], in0=k_sb[:, t, :], scalar=-period, in1=banks[t][:], op0=ALU.mult, op1=ALU.add
+                )
+
+            count(0)
+            for t in range(1, 4):
+                count(t)
+                rest(t - 1)
+            if side == "q":
+                signed = work.tile([P, 4, HALF], I32, name="signed", align_bytes=64)
+                rest(3)
+                nc.vector.scalar_tensor_tensor(
+                    out=signed[:], in0=k_sb[:], scalar=31,
+                    in1=a32[:].bitcast(I32)[:, g, :].unsqueeze(2).to_broadcast([P, 4, HALF]),
+                    op0=ALU.logical_shift_left, op1=ALU.bitwise_xor,
+                )
+                state[ch, "amp"] = signed[:].bitcast(F32).rearrange("p t n -> p n t")
+            else:
+                rest(3)
+                state[ch, "amp"] = vec["c"][:, g, :].unsqueeze(1).to_broadcast([P, HALF, 4])
+            state[ch, "r"] = r_sb
+
+        def waves(ch):
+            side, h, g = ch
+            r_sb = state[ch, "r"]
+            for part in ("im", "re"):
+                s_sb = work.tile([P, 4, HALF], F32, name="s_sb", bufs=4, align_bytes=64)
+                if side == "q":
+                    nc.scalar.activation(out=s_sb[:], in_=r_sb[:], func=ACTF.Sin, bias=0.0 if part == "im" else half_pi[:])
+                else:
+                    w_sb = work.tile([P, 4, HALF], F32, name="w_sb", align_bytes=64)
+                    for t in range(4):
+                        bias = (role_s if part == "im" else role_c)[:, g, t : t + 1]
+                        nc.scalar.activation(out=w_sb[:, t, :], in_=r_sb[:, t, :], func=ACTF.Abs, bias=bias)
+                    nc.scalar.activation(out=s_sb[:], in_=w_sb[:], func=ACTF.Sin, scale=-1.0, bias=half_pi[:])
+                state[ch, part] = s_sb
+
+        def scale(ch, part, eng):
+            ph = work.tile([P, HALF, 4], BF16, name=f"ph_{part}", align_bytes=64)
+            eng.tensor_tensor(
+                out=ph[:], in0=state[ch, part][:].rearrange("p t n -> p n t"), in1=state[ch, "amp"], op=ALU.mult
+            )
+            state[ch, part, "ph"] = ph
+
+        def quantize(ch, part):
+            side, h, g = ch
+            pc = keep.tile([P, HALF], U32, name=f"pc_{side}{h}{g}{part}", align_bytes=64)
+            psc = keep.tile([P, HALF], U8, name=f"psc_{side}{h}{g}{part}", align_bytes=64)
+            nc.vector.quantize_mx(
+                out=pc[:].bitcast(FP8X4), scales=psc[:], in_=state[ch, part, "ph"][:].rearrange("p n t -> p (n t)")
+            )
+            phasor[side, h, g, part] = (pc, psc)
+
+        def passes(acc, qi, kh, g, first, last):
+            qh, qs = qi // 4, slice(P * (qi % 4), P * (qi % 4) + P)
+            for part in ("im", "re"):
+                lc, ls = phasor["q", qh, g, part]
+                rc, rs = phasor["k", kh, g, part]
+                nc.tensor.matmul_mx(
+                    out=acc[:], lhsT=lc[:, qs].bitcast(FP8X4), lhsT_scale=ls[:, qs],
+                    rhs=rc[:].bitcast(FP8X4), rhs_scale=rs[:], start=first and part == "im", stop=last and part == "re",
+                )
+
+        def leave(acc, qi, kh, eng):
+            o_sb = work.tile([P, HALF], F32, name="o_sb", bufs=4, align_bytes=64)
+            if eng == "v":
+                nc.vector.tensor_scalar(o_sb[:], acc[:], 1.0 / 32.0, None, op0=ALU.mult)
+            else:
+                nc.scalar.activation(out=o_sb[:], in_=acc[:], func=ACTF.Copy, scale=1.0 / 32.0)
+            nc.sync.dma_start(out=out[P * qi : P * qi + P, HALF * kh : HALF * kh + HALF], in_=o_sb[:])
+
+        def product(qi, kh, eng="s"):
+            acc = psum.tile([P, HALF], F32, name="acc", tag="acc")
+            passes(acc, qi, kh, 0, True, False)
+            passes(acc, qi, kh, 1, False, True)
+            leave(acc, qi, kh, eng)
+
+        order = [("q", 0, 0), ("k", 0, 0), ("q", 0, 1), ("k", 0, 1), ("q", 1, 0), ("k", 1, 0), ("q", 1, 1), ("k", 1, 1)]
+        copies = (nc.scalar.copy, nc.vector.tensor_copy)
+
+        turn("q", 0, x_sb[0], copies)
+        weights()
+        constants()
+        yb0 = widen(0)
+        matmuls(order[0])
+        for n, ch in enumerate(order):
+            prev = order[n - 1] if n else None
+            reduce(ch)
+            if prev:
+                scale(prev, "im", nc.gpsimd)
+            if n + 1 < len(order):
+                if n == 0:
+                    turn("k", 0, yb0, copies)
+                if n == 2:
+                    turn("q", 1, x_sb[1], copies)
+                if n == 4:
+                    turn("k", 1, yb1, copies)
+                matmuls(order[n + 1])
+            if prev:
+                scale(prev, "re", nc.vector)
+                quantize(prev, "im")
+                quantize(prev, "re")
+            waves(ch)
+            if n == 2:
+                yb1 = widen(1)
+            if n == 4:
+                for qi in range(4):
+                    product(qi, 0)
+            if n == 7:
+                for qi in range(4, 8):
+                    product(qi, 0)
+        last = order[-1]
+        scale(last, "im", nc.gpsimd)
+        scale(last, "re", nc.vector)
+        quantize(last, "im")
+        quantize(last, "re")
+        accs = []
+        for qi in range(8):
+            acc = psum.tile([P, HALF], F32, name="acc2", tag="acc" if qi % 2 == 0 else "ps")
+            passes(acc, qi, 1, 0, True, False)
+            accs.append(acc)
+        for qi in range(8):
+            passes(accs[qi], qi, 1, 1, False, True)
+            leave(accs[qi], qi, 1, "sv"[qi % 2])

@@ -166,10 +166,10 @@ def tile_fhrrbounditemsimilarity_d1p_kernel(tc, x, y_bytes, y_scale, w_words, w_
                     in1=a32[:].bitcast(I32)[:, g, :].unsqueeze(2).to_broadcast([P, 4, HALF]),
                     op0=ALU.logical_shift_left, op1=ALU.bitwise_xor,
                 )
-                state[ch, "amp"] = signed[:].bitcast(F32).rearrange("p t n -> p n t")
+                state[ch, "amp"] = signed[:].bitcast(F32).rearrange("p t (c i) -> p c t i", i=4)
             else:
                 rest(3)
-                state[ch, "amp"] = vec["c"][:, g, :].unsqueeze(1).to_broadcast([P, HALF, 4])
+                state[ch, "amp"] = vec["c"][:, g, :].unsqueeze(1).unsqueeze(3).to_broadcast([P, HALF // 4, 4, 4])
             state[ch, "r"] = r_sb
 
         def waves(ch):
@@ -190,7 +190,8 @@ def tile_fhrrbounditemsimilarity_d1p_kernel(tc, x, y_bytes, y_scale, w_words, w_
         def scale(ch, part, eng):
             ph = work.tile([P, HALF, 4], BF16, name=f"ph_{part}", align_bytes=64)
             eng.tensor_tensor(
-                out=ph[:], in0=state[ch, part][:].rearrange("p t n -> p n t"), in1=state[ch, "amp"], op=ALU.mult
+                out=ph[:].rearrange("p (c i) t -> p c t i", i=4), in0=state[ch, part][:].rearrange("p t (c i) -> p c t i", i=4),
+                in1=state[ch, "amp"], op=ALU.mult,
             )
             state[ch, part, "ph"] = ph
 

@@ -20,6 +20,10 @@ D = 512
 FREQ = 1024
 HALF = 512
 PI = math.pi
+ORDER = [("q", 0, 0, 0, 512), ("k", 0, 0, 0, 512), ("q", 0, 1, 0, 512), ("k", 0, 1, 0, 512), ("k", 1, 0, 0, 512),
+         ("k", 1, 1, 0, 512), ("q", 1, 0, 0, 512), ("q", 1, 1, 0, 256), ("q", 1, 1, 256, 256)]
+KIND = dict(zip(ORDER, "PAAPAAPPP"))
+G_SHARE = {}
 FLOPS = 2 * 2 * TOK * D * FREQ + 2 * 2 * TOK * TOK * FREQ
 
 
@@ -60,55 +64,71 @@ def tile_fhrrbounditemsimilarity_d1p_kernel(tc, x, y_bytes, y_scale, w_words, w_
             nc.sync.dma_start(out=x_sb[0][:, 2 * b : 2 * b + 2, :], in_=xv[0][:, 2 * b : 2 * b + 2, :])
         for q in range(4):
             nc.sync.dma_start(out=wsraw[32 * q : 32 * q + 4, :].bitcast(I32), in_=w_scales[0, 4 * q : 4 * q + 4, :].bitcast(I32))
-        nc.sync.dma_start(out=wraw[:].bitcast(I32), in_=w_words[0].rearrange("p n t -> p (n t)").bitcast(I32))
-        nc.sync.dma_start(out=y_sb[0][:], in_=yv[0])
+        wv = w_words[0].rearrange("p n t -> p (n t)").bitcast(I32)
+        for g in range(2):
+            nc.sync.dma_start(out=wraw[:, 512 * g : 512 * g + 512].bitcast(I32), in_=wv[:, 512 * g : 512 * g + 512])
+            if g == 0:
+                nc.sync.dma_start(out=y_sb[0][:], in_=yv[0])
         nc.sync.dma_start(out=x_sb[1][:], in_=xv[1])
         nc.sync.dma_start(out=y_sb[1][:], in_=yv[1])
 
         half_pi = keep.tile([P, 1], F32, name="half_pi")
         nc.vector.tensor_scalar(half_pi[:], zero[:], PI / 2, None, op0=ALU.add)
+        neg_half_pi = keep.tile([P, 1], F32, name="neg_half_pi")
+        nc.vector.tensor_scalar(neg_half_pi[:], zero[:], -PI / 2, None, op0=ALU.add)
         warm = keep.tile([P, 1], F32, name="warm")
         nc.scalar.activation(out=warm[:], in_=zero[:], func=ACTF.Sin)
+        a32 = keep.tile([P, 2, 4], F32, name="a32")
+        role_a = keep.tile([P, 2, 4], F32, name="role_a")
+        role_n = keep.tile([P, 2, 4], F32, name="role_n")
         role_k = keep.tile([P, 2, 4], F32, name="role_k")
         role_s = keep.tile([P, 2, 4], F32, name="role_s")
         role_c = keep.tile([P, 2, 4], F32, name="role_c")
-        a32 = keep.tile([P, 2, 4], F32, name="a32")
+        c32 = keep.tile([P, 2, 4], F32, name="c32")
 
         wp = keep.tile([P, FREQ], U32, name="wp", align_bytes=64)
         wsp = keep.tile([P, FREQ], U8, name="wsp", align_bytes=64)
 
-        def weights():
+        def weights(g):
+            cols = slice(512 * g, 512 * g + 512)
             nc.vector.tensor_copy(
-                out=wp[:].bitcast(I32).rearrange("p (g t m) -> p g t m", g=2, t=4),
-                in_=wraw[:].bitcast(I32).rearrange("p (g m t) -> p g t m", g=2, t=4),
+                out=wsp[:, cols].rearrange("p (t m) -> p t m", t=4), in_=wsraw[:, cols].rearrange("p (m t) -> p t m", t=4)
             )
             nc.vector.tensor_copy(
-                out=wsp[:].rearrange("p (g t m) -> p g t m", g=2, t=4),
-                in_=wsraw[:].rearrange("p (g m t) -> p g t m", g=2, t=4),
+                out=wp[:, cols].bitcast(I32).rearrange("p (t m) -> p t m", t=4),
+                in_=wraw[:, cols].bitcast(I32).rearrange("p (m t) -> p t m", t=4),
             )
 
         def constants():
-            nc.vector.tensor_scalar(role_k[:], vec["role"][:], -PI / 4, None, op0=ALU.add)
-            nc.vector.tensor_copy(out=role_c[:], in_=vec["role"][:])
-            nc.vector.tensor_scalar(role_s[:], vec["role"][:], -PI / 2, None, op0=ALU.add)
+            nc.vector.tensor_scalar(role_k[:], vec["role"][:], PI / 4, None, op0=ALU.add)
+            nc.vector.tensor_copy(out=role_s[:], in_=vec["role"][:])
+            nc.vector.tensor_scalar(role_c[:], vec["role"][:], PI / 2, None, op0=ALU.add)
+            nc.vector.tensor_scalar(role_a[:], vec["role"][:], -PI / 4, None, op0=ALU.add)
+            nc.vector.tensor_scalar(role_n[:], vec["role"][:], -PI / 2, None, op0=ALU.add)
+            nc.vector.tensor_copy(out=c32[:], in_=vec["c"][:])
             nc.vector.tensor_copy(out=a32[:], in_=vec["a"][:])
 
         codes = {}
+        grouped_of = {}
 
         def turn(side, h, src, engines):
             words = src[:].bitcast(F32)
             grouped = work.tile([P, HALF, 4], BF16, name="grouped", align_bytes=64)
-            flat = grouped[:].rearrange("p n t -> p (n t)")
-            gw = flat.bitcast(F32).rearrange("p (i r u) -> p i r u", i=4, u=2)
+            gw = grouped[:].rearrange("p n t -> p (n t)").bitcast(F32).rearrange("p (i r u) -> p i r u", i=4, u=2)
             for b in range(2):
-                tp = psum.tile([P, 2, 2, P], F32, name="tp", tag="ps")
+                tp = psum.tile([P, 2, 2, P], F32, name="tp", tag="acc")
                 for i in range(2):
                     for u in range(2):
                         nc.tensor.transpose(tp[:, i, u, :], words[:, 2 * b + i, u : D // 2 : 2], ident[:])
                 engines[b](out=gw[:, 2 * b : 2 * b + 2], in_=tp[:].rearrange("p i u r -> p i r u"))
+            grouped_of[side, h] = grouped
+
+        def quantize_input(side, h):
             cd = keep.tile([P, HALF], U32, name=f"in_codes_{side}{h}", align_bytes=64)
             sc = keep.tile([P, HALF], U8, name=f"in_scales_{side}{h}", align_bytes=64)
-            nc.vector.quantize_mx(out=cd[:].bitcast(FP8X4), scales=sc[:], in_=flat)
+            nc.vector.quantize_mx(
+                out=cd[:].bitcast(FP8X4), scales=sc[:], in_=grouped_of[side, h][:].rearrange("p n t -> p (n t)")
+            )
             codes[side, h] = (cd, sc)
 
         def widen(h):
@@ -125,153 +145,222 @@ def tile_fhrrbounditemsimilarity_d1p_kernel(tc, x, y_bytes, y_scale, w_words, w_
         state = {}
 
         def matmuls(ch):
-            side, h, g = ch
+            side, h, g, n0, n = ch
             cd, sc = codes[side, h]
             banks = []
             for t in range(4):
                 ps = psum.tile([P, HALF], F32, name="ps", tag="ps")
                 col = slice((4 * g + t) * P, (4 * g + t + 1) * P)
                 nc.tensor.matmul_mx(
-                    out=ps[:], lhsT=wp[:, col].bitcast(FP8X4), lhsT_scale=wsp[:, col],
-                    rhs=cd[:].bitcast(FP8X4), rhs_scale=sc[:], start=True, stop=True,
+                    out=ps[:, :n], lhsT=wp[:, col].bitcast(FP8X4), lhsT_scale=wsp[:, col],
+                    rhs=cd[:, n0 : n0 + n].bitcast(FP8X4), rhs_scale=sc[:, n0 : n0 + n], start=True, stop=True,
                 )
                 banks.append(ps)
             state[ch, "banks"] = banks
 
         def reduce(ch):
-            side, h, g = ch
+            side, h, g, n0, n = ch
             banks = state[ch, "banks"]
             k_sb = work.tile([P, 4, HALF], I32, name="k_sb", align_bytes=64)
             r_sb = work.tile([P, 4, HALF], F32, name="r_sb", align_bytes=64)
-            period = PI if side == "q" else 2 * PI
+            period = PI if KIND[ch] == "P" else 2 * PI
 
             def count(t):
-                off = PI / 4 if side == "q" else role_k[:, g, t : t + 1]
-                nc.vector.tensor_scalar(k_sb[:, t, :], banks[t][:], off, 1.0 / period, op0=ALU.add, op1=ALU.mult)
+                if side == "q":
+                    off = PI / 4 if KIND[ch] == "P" else -PI / 4
+                else:
+                    off = (role_k if KIND[ch] == "P" else role_a)[:, g, t : t + 1]
+                nc.vector.tensor_scalar(k_sb[:, t, :n], banks[t][:, :n], off, 1.0 / period, op0=ALU.add, op1=ALU.mult)
 
             def rest(t):
                 nc.vector.scalar_tensor_tensor(
-                    out=r_sb[:, t, :], in0=k_sb[:, t, :], scalar=-period, in1=banks[t][:], op0=ALU.mult, op1=ALU.add
+                    out=r_sb[:, t, :n], in0=k_sb[:, t, :n], scalar=-period, in1=banks[t][:, :n], op0=ALU.mult, op1=ALU.add
                 )
 
             count(0)
             for t in range(1, 4):
                 count(t)
                 rest(t - 1)
-            if side == "q":
+            rest(3)
+            state[ch, "r"] = r_sb
+            state[ch, "k"] = k_sb
+
+        def amplitude(ch):
+            side, h, g, n0, n = ch
+            if KIND[ch] == "P":
                 signed = work.tile([P, 4, HALF], I32, name="signed", align_bytes=64)
-                rest(3)
                 nc.vector.scalar_tensor_tensor(
-                    out=signed[:], in0=k_sb[:], scalar=31,
-                    in1=a32[:].bitcast(I32)[:, g, :].unsqueeze(2).to_broadcast([P, 4, HALF]),
+                    out=signed[:, :, :n], in0=state[ch, "k"][:, :, :n], scalar=31,
+                    in1=(c32 if side == "k" else a32)[:].bitcast(I32)[:, g, :].unsqueeze(2).to_broadcast([P, 4, n]),
                     op0=ALU.logical_shift_left, op1=ALU.bitwise_xor,
                 )
-                state[ch, "amp"] = signed[:].bitcast(F32).rearrange("p t (c i) -> p c t i", i=4)
+                state[ch, "amp"] = signed[:, :, :n].bitcast(F32).rearrange("p t (c i) -> p c t i", i=4)
             else:
-                rest(3)
-                state[ch, "amp"] = vec["c"][:, g, :].unsqueeze(1).unsqueeze(3).to_broadcast([P, HALF // 4, 4, 4])
-            state[ch, "r"] = r_sb
+                camp = work.tile([P, 4], F32, name="camp")
+                nc.vector.tensor_copy(out=camp[:], in_=vec["a" if side == "q" else "c"][:, g, :])
+                state[ch, "amp"] = camp[:].unsqueeze(1).unsqueeze(3).to_broadcast([P, n // 4, 4, 4])
 
         def waves(ch):
-            side, h, g = ch
+            side, h, g, n0, n = ch
             r_sb = state[ch, "r"]
             for part in ("im", "re"):
                 s_sb = work.tile([P, 4, HALF], F32, name="s_sb", bufs=4, align_bytes=64)
-                if side == "q":
-                    nc.scalar.activation(out=s_sb[:], in_=r_sb[:], func=ACTF.Sin, bias=0.0 if part == "im" else half_pi[:])
+                if KIND[ch] == "P":
+                    if side == "q":
+                        nc.scalar.activation(out=s_sb[:, :, :n], in_=r_sb[:, :, :n], func=ACTF.Sin, bias=0.0 if part == "im" else half_pi[:])
+                    else:
+                        for t in range(4):
+                            bias = (role_s if part == "im" else role_c)[:, g, t : t + 1]
+                            nc.scalar.activation(out=s_sb[:, t, :n], in_=r_sb[:, t, :n], func=ACTF.Sin, bias=bias)
                 else:
                     w_sb = work.tile([P, 4, HALF], F32, name="w_sb", align_bytes=64)
-                    for t in range(4):
-                        bias = (role_s if part == "im" else role_c)[:, g, t : t + 1]
-                        nc.scalar.activation(out=w_sb[:, t, :], in_=r_sb[:, t, :], func=ACTF.Abs, bias=bias)
-                    nc.scalar.activation(out=s_sb[:], in_=w_sb[:], func=ACTF.Sin, scale=-1.0, bias=half_pi[:])
+                    if side == "q":
+                        nc.scalar.activation(out=w_sb[:, :, :n], in_=r_sb[:, :, :n], func=ACTF.Abs, bias=0.0 if part == "re" else neg_half_pi[:])
+                    else:
+                        for t in range(4):
+                            bias = (role_n if part == "im" else role_s)[:, g, t : t + 1]
+                            nc.scalar.activation(out=w_sb[:, t, :n], in_=r_sb[:, t, :n], func=ACTF.Abs, bias=bias)
+                    nc.scalar.activation(out=s_sb[:, :, :n], in_=w_sb[:, :, :n], func=ACTF.Sin, scale=-1.0, bias=half_pi[:])
                 state[ch, part] = s_sb
 
-        def scale(ch, part, eng):
-            ph = work.tile([P, HALF, 4], BF16, name=f"ph_{part}", align_bytes=64)
+        def scale(ch, part, eng, lo=0, hi=None):
+            n = ch[4]
+            hi = n if hi is None else hi
+            if lo == 0:
+                ph = work.tile([P, HALF, 4], BF16, name=f"ph_{part}", align_bytes=64)
+                state[ch, part, "ph"] = ph
+            ph = state[ch, part, "ph"]
+            c0, c1 = lo // 4, hi // 4
             eng.tensor_tensor(
-                out=ph[:].rearrange("p (c i) t -> p c t i", i=4), in0=state[ch, part][:].rearrange("p t (c i) -> p c t i", i=4),
-                in1=state[ch, "amp"], op=ALU.mult,
+                out=ph[:, :n].rearrange("p (c i) t -> p c t i", i=4)[:, c0:c1],
+                in0=state[ch, part][:, :, :n].rearrange("p t (c i) -> p c t i", i=4)[:, c0:c1],
+                in1=state[ch, "amp"][:, c0:c1], op=ALU.mult,
             )
-            state[ch, part, "ph"] = ph
 
         def quantize(ch, part):
-            side, h, g = ch
-            pc = keep.tile([P, HALF], U32, name=f"pc_{side}{h}{g}{part}", align_bytes=64)
-            psc = keep.tile([P, HALF], U8, name=f"psc_{side}{h}{g}{part}", align_bytes=64)
+            side, h, g, n0, n = ch
+            if (side, h, g, part) not in phasor:
+                pc = keep.tile([P, HALF], U32, name=f"pc_{side}{h}{g}{part}", align_bytes=64)
+                psc = keep.tile([P, HALF], U8, name=f"psc_{side}{h}{g}{part}", align_bytes=64)
+                phasor[side, h, g, part] = (pc, psc)
+            pc, psc = phasor[side, h, g, part]
             nc.vector.quantize_mx(
-                out=pc[:].bitcast(FP8X4), scales=psc[:], in_=state[ch, part, "ph"][:].rearrange("p n t -> p (n t)")
+                out=pc[:, n0 : n0 + n].bitcast(FP8X4), scales=psc[:, n0 : n0 + n],
+                in_=state[ch, part, "ph"][:, :n].rearrange("p n t -> p (n t)"),
             )
-            phasor[side, h, g, part] = (pc, psc)
 
-        def passes(acc, qi, kh, g, first, last):
+        def passes(dst, qi, kh, g, n0, n, first, last):
             qh, qs = qi // 4, slice(P * (qi % 4), P * (qi % 4) + P)
             for part in ("im", "re"):
                 lc, ls = phasor["q", qh, g, part]
                 rc, rs = phasor["k", kh, g, part]
                 nc.tensor.matmul_mx(
-                    out=acc[:], lhsT=lc[:, qs].bitcast(FP8X4), lhsT_scale=ls[:, qs],
-                    rhs=rc[:].bitcast(FP8X4), rhs_scale=rs[:], start=first and part == "im", stop=last and part == "re",
+                    out=dst, lhsT=lc[:, qs].bitcast(FP8X4), lhsT_scale=ls[:, qs],
+                    rhs=rc[:, n0 : n0 + n].bitcast(FP8X4), rhs_scale=rs[:, n0 : n0 + n],
+                    start=first and part == "im", stop=last and part == "re",
                 )
 
-        def leave(acc, qi, kh, eng):
-            o_sb = work.tile([P, HALF], F32, name="o_sb", bufs=4, align_bytes=64)
+        def leave(acc, qi, col, n, eng):
+            o_sb = work.tile([P, HALF], F32, name="o_sb", bufs=8, align_bytes=64)
             if eng == "v":
-                nc.vector.tensor_scalar(o_sb[:], acc[:], 1.0 / 32.0, None, op0=ALU.mult)
+                nc.vector.tensor_scalar(o_sb[:, :n], acc[:, :n], 1.0 / 32.0, None, op0=ALU.mult)
             else:
-                nc.scalar.activation(out=o_sb[:], in_=acc[:], func=ACTF.Copy, scale=1.0 / 32.0)
-            nc.sync.dma_start(out=out[P * qi : P * qi + P, HALF * kh : HALF * kh + HALF], in_=o_sb[:])
+                nc.scalar.activation(out=o_sb[:, :n], in_=acc[:, :n], func=ACTF.Copy, scale=1.0 / 32.0)
+            nc.sync.dma_start(out=out[P * qi : P * qi + P, col : col + n], in_=o_sb[:, :n])
 
-        def product(qi, kh, eng="s"):
+        def product(qi, kh, n0=0, n=HALF, eng="s"):
             acc = psum.tile([P, HALF], F32, name="acc", tag="acc")
-            passes(acc, qi, kh, 0, True, False)
-            passes(acc, qi, kh, 1, False, True)
-            leave(acc, qi, kh, eng)
+            passes(acc[:, :n], qi, kh, 0, n0, n, True, False)
+            passes(acc[:, :n], qi, kh, 1, n0, n, False, True)
+            leave(acc, qi, HALF * kh + n0, n, eng)
 
-        order = [("q", 0, 0), ("k", 0, 0), ("q", 0, 1), ("k", 0, 1), ("q", 1, 0), ("k", 1, 0), ("q", 1, 1), ("k", 1, 1)]
-        copies = (nc.scalar.copy, nc.vector.tensor_copy)
+        order = ORDER
+        ss = (nc.scalar.copy, nc.scalar.copy)
+        yb = {}
+        accs = {}
 
-        turn("q", 0, x_sb[0], copies)
-        weights()
-        constants()
-        yb0 = widen(0)
+        def multiply(qi, kh, tag="acc"):
+            acc = psum.tile([P, HALF], F32, name="acc", tag=tag)
+            passes(acc[:], qi, kh, 0, 0, HALF, True, False)
+            passes(acc[:], qi, kh, 1, 0, HALF, False, True)
+            accs[qi, kh] = acc
+
+        def leave_tile(qi, kh, eng):
+            leave(accs[qi, kh], qi, HALF * kh, HALF, eng)
+
+        turn("q", 0, x_sb[0], (nc.scalar.copy, nc.vector.tensor_copy))
+        weights(0)
+        quantize_input("q", 0)
+        yb[0] = widen(0)
         matmuls(order[0])
+        constants()
         for n, ch in enumerate(order):
             prev = order[n - 1] if n else None
             reduce(ch)
             if prev:
-                scale(prev, "im", nc.gpsimd)
-            if n + 1 < len(order):
-                if n == 0:
-                    turn("k", 0, yb0, copies)
-                if n == 2:
-                    turn("q", 1, x_sb[1], copies)
-                if n == 4:
-                    turn("k", 1, yb1, copies)
-                matmuls(order[n + 1])
+                share = G_SHARE.get(n - 1, prev[4])
+                if share:
+                    scale(prev, "im", nc.gpsimd, 0, share)
+            if n == 7:
+                for qi in range(4):
+                    leave_tile(qi, 1, "v")
+            if n == 0:
+                turn("k", 0, yb[0], (nc.scalar.copy, nc.vector.tensor_copy))
+                weights(1)
+                quantize_input("k", 0)
+            if n == 2:
+                turn("k", 1, yb[1], ss)
+            if n == 4:
+                turn("q", 1, x_sb[1], ss)
             if prev:
                 scale(prev, "re", nc.vector)
-                quantize(prev, "im")
-                quantize(prev, "re")
-            waves(ch)
+                if share < prev[4]:
+                    scale(prev, "im", nc.vector, share, prev[4])
+                    quantize(prev, "re")
+                    quantize(prev, "im")
+                else:
+                    quantize(prev, "im")
+                    quantize(prev, "re")
             if n == 2:
-                yb1 = widen(1)
+                quantize_input("k", 1)
+            if n == 4:
+                quantize_input("q", 1)
+            amplitude(ch)
+            if n + 1 < len(order):
+                matmuls(order[n + 1])
+            if n == 8:
+                for qi in (4, 5):
+                    for kh in range(2):
+                        acc = psum.tile([P, HALF], F32, name="acc", tag="acc")
+                        passes(acc[:], qi, kh, 0, 0, HALF, True, False)
+                        accs[qi, kh] = acc
+            waves(ch)
+            if n == 0:
+                yb[1] = widen(1)
             if n == 4:
                 for qi in range(4):
-                    product(qi, 0)
-            if n == 7:
-                for qi in range(4, 8):
-                    product(qi, 0)
+                    multiply(qi, 0)
+            if n == 5:
+                for qi in range(4):
+                    leave_tile(qi, 0, "s")
+            if n == 6:
+                for qi in range(4):
+                    multiply(qi, 1)
         last = order[-1]
-        scale(last, "im", nc.gpsimd)
+        tail = [(6, 0), (6, 1), (7, 0), (7, 1)]
+        for qi, kh in tail:
+            acc = psum.tile([P, HALF], F32, name="acc2", tag="ps")
+            passes(acc[:], qi, kh, 0, 0, HALF, True, False)
+            accs[qi, kh] = acc
+        for qi in (4, 5):
+            for kh in range(2):
+                passes(accs[qi, kh][:], qi, kh, 1, 0, HALF, False, True)
+        scale(last, "im", nc.vector)
         scale(last, "re", nc.vector)
         quantize(last, "im")
         quantize(last, "re")
-        accs = []
-        for qi in range(8):
-            acc = psum.tile([P, HALF], F32, name="acc2", tag="acc" if qi % 2 == 0 else "ps")
-            passes(acc, qi, 1, 0, True, False)
-            accs.append(acc)
-        for qi in range(8):
-            passes(accs[qi], qi, 1, 1, False, True)
-            leave(accs[qi], qi, 1, "sv"[qi % 2])
+        for m, (qi, kh) in enumerate([(4, 0), (4, 1), (5, 0), (5, 1)]):
+            leave_tile(qi, kh, "sssv"[m])
+        for m, (qi, kh) in enumerate(tail):
+            passes(accs[qi, kh][:], qi, kh, 1, 0, HALF, False, True)
+            leave_tile(qi, kh, "vs"[m % 2])

@@ -20,10 +20,11 @@ D = 512
 FREQ = 1024
 HALF = 512
 PI = math.pi
-ORDER = [("q", 0, 0, 0, 512), ("k", 0, 0, 0, 512), ("q", 0, 1, 0, 512), ("k", 0, 1, 0, 512), ("k", 1, 0, 0, 512),
-         ("k", 1, 1, 0, 512), ("q", 1, 0, 0, 512), ("q", 1, 1, 0, 256), ("q", 1, 1, 256, 256)]
-KIND = dict(zip(ORDER, "PAAPAAPPP"))
-G_SHARE = {}
+ORDER = [("q", 0, 0, 0, 256), ("q", 0, 0, 256, 256), ("k", 0, 0, 0, 512), ("q", 0, 1, 0, 512), ("k", 0, 1, 0, 512), ("k", 1, 0, 0, 512),
+         ("k", 1, 1, 0, 512), ("q", 1, 0, 0, 256), ("q", 1, 1, 0, 256), ("q", 1, 0, 256, 256), ("q", 1, 1, 256, 128), ("q", 1, 1, 384, 128)]
+LEAVES = {7: [(0, 1, 's'), (1, 0, 'v'), (2, 0, 'v'), (3, 0, 'v'), (3, 1, 's')], 8: [(0, 0, 'v')], 9: [(1, 1, 'v'), (2, 1, 'v')], 10: [(4, 1, 's'), (5, 0, 'v')], 11: [(4, 0, 'v'), (5, 1, 'v')]}
+KIND = dict(zip(ORDER, "PAPAPAAAAAAA"))
+G_SHARE = {0: (224, 0), 1: (256, 128), 2: (448, 0), 3: (512, 128), 4: (448, 0), 5: (512, 128), 6: (512, 128), 7: (256, 96), 8: (256, 96), 10: (128, 48)}
 FLOPS = 2 * 2 * TOK * D * FREQ + 2 * 2 * TOK * TOK * FREQ
 
 
@@ -37,6 +38,8 @@ def tile_fhrrbounditemsimilarity_d1p_kernel(tc, x, y_bytes, y_scale, w_words, w_
 
         ident = keep.tile([P, P], F32, name="ident")
         make_identity(nc, ident[:])
+        ident16 = keep.tile([P, P], BF16, name="ident16")
+        make_identity(nc, ident16[:])
         zero = keep.tile([P, 1], F32, name="zero")
         nc.vector.memset(zero[:], 0.0)
         wsraw = keep.tile([P, FREQ], U8, name="wsraw", align_bytes=64)
@@ -60,15 +63,14 @@ def tile_fhrrbounditemsimilarity_d1p_kernel(tc, x, y_bytes, y_scale, w_words, w_
             x_sb.append(xt)
             y_sb.append(yt)
         wraw = keep.tile([P, FREQ], U32, name="wraw", align_bytes=64)
-        for b in range(2):
-            nc.sync.dma_start(out=x_sb[0][:, 2 * b : 2 * b + 2, :], in_=xv[0][:, 2 * b : 2 * b + 2, :])
+        wv = w_words[0].rearrange("p n t -> p (n t)").bitcast(I32)
+        nc.sync.dma_start(out=x_sb[0][:, 0:2, :], in_=xv[0][:, 0:2, :])
         for q in range(4):
             nc.sync.dma_start(out=wsraw[32 * q : 32 * q + 4, :].bitcast(I32), in_=w_scales[0, 4 * q : 4 * q + 4, :].bitcast(I32))
-        wv = w_words[0].rearrange("p n t -> p (n t)").bitcast(I32)
-        for g in range(2):
-            nc.sync.dma_start(out=wraw[:, 512 * g : 512 * g + 512].bitcast(I32), in_=wv[:, 512 * g : 512 * g + 512])
-            if g == 0:
-                nc.sync.dma_start(out=y_sb[0][:], in_=yv[0])
+        nc.sync.dma_start(out=wraw[:, 0:512].bitcast(I32), in_=wv[:, 0:512])
+        nc.sync.dma_start(out=x_sb[0][:, 2:4, :], in_=xv[0][:, 2:4, :])
+        nc.sync.dma_start(out=y_sb[0][:], in_=yv[0])
+        nc.sync.dma_start(out=wraw[:, 512:1024].bitcast(I32), in_=wv[:, 512:1024])
         nc.sync.dma_start(out=x_sb[1][:], in_=xv[1])
         nc.sync.dma_start(out=y_sb[1][:], in_=yv[1])
 
@@ -99,7 +101,14 @@ def tile_fhrrbounditemsimilarity_d1p_kernel(tc, x, y_bytes, y_scale, w_words, w_
                 in_=wraw[:, cols].bitcast(I32).rearrange("p (m t) -> p t m", t=4),
             )
 
+        amp_ps = psum.tile([P, 2, 2, 4], F32, name="amp_ps", tag="amp", bufs=1)
+
         def constants():
+            for s, v in enumerate("ac"):
+                nc.tensor.matmul(
+                    amp_ps[:, s].rearrange("p g t -> p (g t)"), lhsT=ident16[:], rhs=vec[v][:].rearrange("p g t -> p (g t)"),
+                    start=True, stop=True,
+                )
             nc.vector.tensor_scalar(role_k[:], vec["role"][:], PI / 4, None, op0=ALU.add)
             nc.vector.tensor_copy(out=role_s[:], in_=vec["role"][:])
             nc.vector.tensor_scalar(role_c[:], vec["role"][:], PI / 2, None, op0=ALU.add)
@@ -111,25 +120,27 @@ def tile_fhrrbounditemsimilarity_d1p_kernel(tc, x, y_bytes, y_scale, w_words, w_
         codes = {}
         grouped_of = {}
 
-        def turn(side, h, src, engines):
+        def turn(side, h, b, src, copy):
             words = src[:].bitcast(F32)
-            grouped = work.tile([P, HALF, 4], BF16, name="grouped", align_bytes=64)
-            gw = grouped[:].rearrange("p n t -> p (n t)").bitcast(F32).rearrange("p (i r u) -> p i r u", i=4, u=2)
-            for b in range(2):
-                tp = psum.tile([P, 2, 2, P], F32, name="tp", tag="acc")
-                for i in range(2):
-                    for u in range(2):
-                        nc.tensor.transpose(tp[:, i, u, :], words[:, 2 * b + i, u : D // 2 : 2], ident[:])
-                engines[b](out=gw[:, 2 * b : 2 * b + 2], in_=tp[:].rearrange("p i u r -> p i r u"))
-            grouped_of[side, h] = grouped
+            if b == 0:
+                grouped_of[side, h] = work.tile([P, HALF, 4], BF16, name="grouped", align_bytes=64)
+            gw = grouped_of[side, h][:].rearrange("p n t -> p (n t)").bitcast(F32).rearrange("p (i r u) -> p i r u", i=4, u=2)
+            tp = psum.tile([P, 2, 2, P], F32, name="tp", tag="acc", bufs=3)
+            for i in range(2):
+                for u in range(2):
+                    nc.tensor.transpose(tp[:, i, u, :], words[:, 2 * b + i, u : D // 2 : 2], ident[:])
+            copy(out=gw[:, 2 * b : 2 * b + 2], in_=tp[:].rearrange("p i u r -> p i r u"))
 
-        def quantize_input(side, h):
-            cd = keep.tile([P, HALF], U32, name=f"in_codes_{side}{h}", align_bytes=64)
-            sc = keep.tile([P, HALF], U8, name=f"in_scales_{side}{h}", align_bytes=64)
+        def quantize_input(side, h, n0=0, n=HALF):
+            if n0 == 0:
+                cd = keep.tile([P, HALF], U32, name=f"in_codes_{side}{h}", align_bytes=64)
+                sc = keep.tile([P, HALF], U8, name=f"in_scales_{side}{h}", align_bytes=64)
+                codes[side, h] = (cd, sc)
+            cd, sc = codes[side, h]
             nc.vector.quantize_mx(
-                out=cd[:].bitcast(FP8X4), scales=sc[:], in_=grouped_of[side, h][:].rearrange("p n t -> p (n t)")
+                out=cd[:, n0 : n0 + n].bitcast(FP8X4), scales=sc[:, n0 : n0 + n],
+                in_=grouped_of[side, h][:, n0 : n0 + n].rearrange("p n t -> p (n t)"),
             )
-            codes[side, h] = (cd, sc)
 
         def widen(h):
             yb = work.tile([P, 4, D], BF16, name="y_bf", align_bytes=64)
@@ -198,6 +209,7 @@ def tile_fhrrbounditemsimilarity_d1p_kernel(tc, x, y_bytes, y_scale, w_words, w_
             else:
                 camp = work.tile([P, 4], F32, name="camp")
                 nc.vector.tensor_copy(out=camp[:], in_=vec["a" if side == "q" else "c"][:, g, :])
+                state[ch, "amp_v"] = amp_ps[:, "qk".index(side), g, :].unsqueeze(1).unsqueeze(3).to_broadcast([P, n // 4, 4, 4])
                 state[ch, "amp"] = camp[:].unsqueeze(1).unsqueeze(3).to_broadcast([P, n // 4, 4, 4])
 
         def waves(ch):
@@ -226,7 +238,7 @@ def tile_fhrrbounditemsimilarity_d1p_kernel(tc, x, y_bytes, y_scale, w_words, w_
         def scale(ch, part, eng, lo=0, hi=None):
             n = ch[4]
             hi = n if hi is None else hi
-            if lo == 0:
+            if (ch, part, "ph") not in state:
                 ph = work.tile([P, HALF, 4], BF16, name=f"ph_{part}", align_bytes=64)
                 state[ch, part, "ph"] = ph
             ph = state[ch, part, "ph"]
@@ -234,7 +246,7 @@ def tile_fhrrbounditemsimilarity_d1p_kernel(tc, x, y_bytes, y_scale, w_words, w_
             eng.tensor_tensor(
                 out=ph[:, :n].rearrange("p (c i) t -> p c t i", i=4)[:, c0:c1],
                 in0=state[ch, part][:, :, :n].rearrange("p t (c i) -> p c t i", i=4)[:, c0:c1],
-                in1=state[ch, "amp"][:, c0:c1], op=ALU.mult,
+                in1=state[ch, "amp_v" if eng is nc.vector and KIND[ch] == "A" else "amp"][:, c0:c1], op=ALU.mult,
             )
 
         def quantize(ch, part):
@@ -275,92 +287,93 @@ def tile_fhrrbounditemsimilarity_d1p_kernel(tc, x, y_bytes, y_scale, w_words, w_
             leave(acc, qi, HALF * kh + n0, n, eng)
 
         order = ORDER
-        ss = (nc.scalar.copy, nc.scalar.copy)
-        yb = {}
+        sc, vc = nc.scalar.copy, nc.vector.tensor_copy
         accs = {}
 
-        def multiply(qi, kh, tag="acc"):
-            acc = psum.tile([P, HALF], F32, name="acc", tag=tag)
+        def start(qi, kh, tag):
+            acc = psum.tile([P, HALF], F32, name="acc", tag=tag, bufs=3 if tag == "acc" else 4)
             passes(acc[:], qi, kh, 0, 0, HALF, True, False)
-            passes(acc[:], qi, kh, 1, 0, HALF, False, True)
             accs[qi, kh] = acc
+
+        def finish(qi, kh):
+            passes(accs[qi, kh][:], qi, kh, 1, 0, HALF, False, True)
 
         def leave_tile(qi, kh, eng):
             leave(accs[qi, kh], qi, HALF * kh, HALF, eng)
 
-        turn("q", 0, x_sb[0], (nc.scalar.copy, nc.vector.tensor_copy))
+        turn("q", 0, 0, x_sb[0], sc)
         weights(0)
-        quantize_input("q", 0)
-        yb[0] = widen(0)
+        quantize_input("q", 0, 0, 256)
         matmuls(order[0])
         constants()
+        turn("q", 0, 1, x_sb[0], sc)
+        yb0 = widen(0)
+        LASTN = len(order) - 1
         for n, ch in enumerate(order):
             prev = order[n - 1] if n else None
             reduce(ch)
-            if prev:
-                share = G_SHARE.get(n - 1, prev[4])
-                if share:
-                    scale(prev, "im", nc.gpsimd, 0, share)
-            if n == 7:
-                for qi in range(4):
-                    leave_tile(qi, 1, "v")
             if n == 0:
-                turn("k", 0, yb[0], (nc.scalar.copy, nc.vector.tensor_copy))
+                quantize_input("q", 0, 256, 256)
                 weights(1)
+                amplitude(ch)
+                matmuls(order[1])
+                waves(ch)
+                turn("k", 0, 0, yb0, sc)
+                turn("k", 0, 1, yb0, sc)
+                continue
+            share, extra = G_SHARE.get(n - 1, (prev[4], 0))
+            if share:
+                scale(prev, "im", nc.gpsimd, 0, share)
+            if extra:
+                scale(prev, "re", nc.gpsimd, 0, extra)
+            for qi, kh, eng in LEAVES.get(n, []):
+                if eng == "v":
+                    leave_tile(qi, kh, "v")
+            if n == 1:
                 quantize_input("k", 0)
-            if n == 2:
-                turn("k", 1, yb[1], ss)
-            if n == 4:
-                turn("q", 1, x_sb[1], ss)
-            if prev:
-                scale(prev, "re", nc.vector)
-                if share < prev[4]:
-                    scale(prev, "im", nc.vector, share, prev[4])
-                    quantize(prev, "re")
-                    quantize(prev, "im")
-                else:
-                    quantize(prev, "im")
-                    quantize(prev, "re")
-            if n == 2:
+            if n == 3:
+                turn("k", 1, 0, yb1, sc)
+                turn("k", 1, 1, yb1, sc)
+            if n == 5:
+                turn("q", 1, 0, x_sb[1], sc)
+                turn("q", 1, 1, x_sb[1], sc)
+            scale(prev, "re", nc.vector, extra, prev[4])
+            if share < prev[4]:
+                scale(prev, "im", nc.vector, share, prev[4])
+                quantize(prev, "re")
+                quantize(prev, "im")
+            else:
+                quantize(prev, "im")
+                quantize(prev, "re")
+            if n == 3:
                 quantize_input("k", 1)
-            if n == 4:
+            if n == 5:
                 quantize_input("q", 1)
             amplitude(ch)
-            if n + 1 < len(order):
+            if n < LASTN:
                 matmuls(order[n + 1])
-            if n == 8:
-                for qi in (4, 5):
-                    for kh in range(2):
-                        acc = psum.tile([P, HALF], F32, name="acc", tag="acc")
-                        passes(acc[:], qi, kh, 0, 0, HALF, True, False)
-                        accs[qi, kh] = acc
+            for qi, kh, eng in [e for e in LEAVES.get(n, []) if e[2] == "s"] + [e for e in LEAVES.get(n + 1, []) if e[2] == "v"]:
+                start(qi, kh, "acc")
+                finish(qi, kh)
             waves(ch)
-            if n == 0:
-                yb[1] = widen(1)
-            if n == 4:
-                for qi in range(4):
-                    multiply(qi, 0)
-            if n == 5:
-                for qi in range(4):
-                    leave_tile(qi, 0, "s")
-            if n == 6:
-                for qi in range(4):
-                    multiply(qi, 1)
+
+            if n == 1:
+                yb1 = widen(1)
+            for qi, kh, eng in LEAVES.get(n, []):
+                if eng == "s":
+                    leave_tile(qi, kh, "s")
         last = order[-1]
-        tail = [(6, 0), (6, 1), (7, 0), (7, 1)]
-        for qi, kh in tail:
-            acc = psum.tile([P, HALF], F32, name="acc2", tag="ps")
-            passes(acc[:], qi, kh, 0, 0, HALF, True, False)
-            accs[qi, kh] = acc
-        for qi in (4, 5):
+        for qi in (6, 7):
             for kh in range(2):
-                passes(accs[qi, kh][:], qi, kh, 1, 0, HALF, False, True)
+                start(qi, kh, "acc" if (qi, kh) != (7, 1) else "ps")
+        for kh in range(2):
+            finish(6, kh)
         scale(last, "im", nc.vector)
         scale(last, "re", nc.vector)
         quantize(last, "im")
         quantize(last, "re")
-        for m, (qi, kh) in enumerate([(4, 0), (4, 1), (5, 0), (5, 1)]):
-            leave_tile(qi, kh, "sssv"[m])
-        for m, (qi, kh) in enumerate(tail):
-            passes(accs[qi, kh][:], qi, kh, 1, 0, HALF, False, True)
-            leave_tile(qi, kh, "vs"[m % 2])
+        for kh in range(2):
+            leave_tile(6, kh, "vs"[kh])
+        for kh in range(2):
+            finish(7, kh)
+            leave_tile(7, kh, "vs"[kh])

import math
from contextlib import ExitStack

import concourse.mybir as mybir
from concourse.masks import make_identity

F32 = mybir.dt.float32
BF16 = mybir.dt.bfloat16
I32 = mybir.dt.int32
U32 = mybir.dt.uint32
U8 = mybir.dt.uint8
FP8 = mybir.dt.float8_e4m3fn
FP8X4 = mybir.dt.float8_e4m3fn_x4
ALU = mybir.AluOpType
ACTF = mybir.ActivationFunctionType

P = 128
TOK = 1024
D = 512
FREQ = 1024
HALF = 512
PI = math.pi
ORDER = [("q", 0, 0, 0, 256), ("q", 0, 0, 256, 256), ("k", 0, 0, 0, 512), ("q", 0, 1, 0, 512), ("k", 0, 1, 0, 512), ("k", 1, 0, 0, 512),
         ("k", 1, 1, 0, 512), ("q", 1, 0, 0, 256), ("q", 1, 1, 0, 256), ("q", 1, 0, 256, 256), ("q", 1, 1, 256, 128), ("q", 1, 1, 384, 128)]
LEAVES = {7: [(0, 1, 's'), (1, 0, 'v'), (2, 0, 'v'), (3, 0, 'v'), (3, 1, 's')], 8: [(0, 0, 'v')], 9: [(1, 1, 'v'), (2, 1, 'v')], 10: [(4, 1, 's'), (5, 0, 'v')], 11: [(4, 0, 'v'), (5, 1, 'v')]}
KIND = dict(zip(ORDER, "PAPAPAAAAAAA"))
G_SHARE = {0: (224, 0), 1: (256, 128), 2: (448, 0), 3: (512, 128), 4: (448, 0), 5: (512, 128), 6: (512, 128), 7: (256, 96), 8: (256, 96), 10: (128, 48)}
FLOPS = 2 * 2 * TOK * D * FREQ + 2 * 2 * TOK * TOK * FREQ


def tile_fhrrbounditemsimilarity_d1p_kernel(tc, x, y_bytes, y_scale, w_words, w_scales, role, a, c, out):
    nc = tc.nc
    with ExitStack() as ctx:
        keep = ctx.enter_context(tc.tile_pool(name="keep", bufs=1))
        work = ctx.enter_context(tc.tile_pool(name="work", bufs=2))
        psum = ctx.enter_context(tc.psum_pool(name="psum", bufs=4))
        ctx.enter_context(tc.manual_schedule())

        ident = keep.tile([P, P], F32, name="ident")
        make_identity(nc, ident[:])
        ident16 = keep.tile([P, P], BF16, name="ident16")
        make_identity(nc, ident16[:])
        zero = keep.tile([P, 1], F32, name="zero")
        nc.vector.memset(zero[:], 0.0)
        wsraw = keep.tile([P, FREQ], U8, name="wsraw", align_bytes=64)
        nc.vector.memset(wsraw[:].bitcast(I32), 0)

        ysc = keep.tile([P, 8, 4], F32, name="ysc")
        nc.scalar.dma_start(out=ysc[:], in_=y_scale.rearrange("(i p) j -> p i j", p=P))
        vec = {}
        for name, v in (("role", role), ("a", a), ("c", c)):
            t = keep.tile([P, 2, 4], BF16, name=f"vec_{name}")
            nc.scalar.dma_start(out=t[:], in_=v.rearrange("(g p t) -> p g t", g=2, t=4))
            vec[name] = t

        x_sb = []
        y_sb = []
        xv = x.rearrange("(h i p) k -> h p i k", p=P, i=4)
        yv = y_bytes.rearrange("(h i p) k -> h p i k", p=P, i=4)
        for h in range(2):
            xt = keep.tile([P, 4, D], BF16, name=f"x_sb{h}", align_bytes=64)
            yt = keep.tile([P, 4, D], U8, name=f"y_sb{h}", align_bytes=64)
            x_sb.append(xt)
            y_sb.append(yt)
        wraw = keep.tile([P, FREQ], U32, name="wraw", align_bytes=64)
        wv = w_words[0].rearrange("p n t -> p (n t)").bitcast(I32)
        nc.sync.dma_start(out=x_sb[0][:, 0:2, :], in_=xv[0][:, 0:2, :])
        for q in range(4):
            nc.sync.dma_start(out=wsraw[32 * q : 32 * q + 4, :].bitcast(I32), in_=w_scales[0, 4 * q : 4 * q + 4, :].bitcast(I32))
        nc.sync.dma_start(out=wraw[:, 0:512].bitcast(I32), in_=wv[:, 0:512])
        nc.sync.dma_start(out=x_sb[0][:, 2:4, :], in_=xv[0][:, 2:4, :])
        nc.sync.dma_start(out=y_sb[0][:], in_=yv[0])
        nc.sync.dma_start(out=wraw[:, 512:1024].bitcast(I32), in_=wv[:, 512:1024])
        nc.sync.dma_start(out=x_sb[1][:], in_=xv[1])
        nc.sync.dma_start(out=y_sb[1][:], in_=yv[1])

        half_pi = keep.tile([P, 1], F32, name="half_pi")
        nc.vector.tensor_scalar(half_pi[:], zero[:], PI / 2, None, op0=ALU.add)
        neg_half_pi = keep.tile([P, 1], F32, name="neg_half_pi")
        nc.vector.tensor_scalar(neg_half_pi[:], zero[:], -PI / 2, None, op0=ALU.add)
        warm = keep.tile([P, 1], F32, name="warm")
        nc.scalar.activation(out=warm[:], in_=zero[:], func=ACTF.Sin)
        a32 = keep.tile([P, 2, 4], F32, name="a32")
        role_a = keep.tile([P, 2, 4], F32, name="role_a")
        role_n = keep.tile([P, 2, 4], F32, name="role_n")
        role_k = keep.tile([P, 2, 4], F32, name="role_k")
        role_s = keep.tile([P, 2, 4], F32, name="role_s")
        role_c = keep.tile([P, 2, 4], F32, name="role_c")
        c32 = keep.tile([P, 2, 4], F32, name="c32")

        wp = keep.tile([P, FREQ], U32, name="wp", align_bytes=64)
        wsp = keep.tile([P, FREQ], U8, name="wsp", align_bytes=64)

        def weights(g):
            cols = slice(512 * g, 512 * g + 512)
            nc.vector.tensor_copy(
                out=wsp[:, cols].rearrange("p (t m) -> p t m", t=4), in_=wsraw[:, cols].rearrange("p (m t) -> p t m", t=4)
            )
            nc.vector.tensor_copy(
                out=wp[:, cols].bitcast(I32).rearrange("p (t m) -> p t m", t=4),
                in_=wraw[:, cols].bitcast(I32).rearrange("p (m t) -> p t m", t=4),
            )

        amp_ps = psum.tile([P, 2, 2, 4], F32, name="amp_ps", tag="amp", bufs=1)

        def constants():
            for s, v in enumerate("ac"):
                nc.tensor.matmul(
                    amp_ps[:, s].rearrange("p g t -> p (g t)"), lhsT=ident16[:], rhs=vec[v][:].rearrange("p g t -> p (g t)"),
                    start=True, stop=True,
                )
            nc.vector.tensor_scalar(role_k[:], vec["role"][:], PI / 4, None, op0=ALU.add)
            nc.vector.tensor_copy(out=role_s[:], in_=vec["role"][:])
            nc.vector.tensor_scalar(role_c[:], vec["role"][:], PI / 2, None, op0=ALU.add)
            nc.vector.tensor_scalar(role_a[:], vec["role"][:], -PI / 4, None, op0=ALU.add)
            nc.vector.tensor_scalar(role_n[:], vec["role"][:], -PI / 2, None, op0=ALU.add)
            nc.vector.tensor_copy(out=c32[:], in_=vec["c"][:])
            nc.vector.tensor_copy(out=a32[:], in_=vec["a"][:])

        codes = {}
        grouped_of = {}

        def turn(side, h, b, src, copy):
            words = src[:].bitcast(F32)
            if b == 0:
                grouped_of[side, h] = work.tile([P, HALF, 4], BF16, name="grouped", align_bytes=64)
            gw = grouped_of[side, h][:].rearrange("p n t -> p (n t)").bitcast(F32).rearrange("p (i r u) -> p i r u", i=4, u=2)
            tp = psum.tile([P, 2, 2, P], F32, name="tp", tag="acc", bufs=3)
            for i in range(2):
                for u in range(2):
                    nc.tensor.transpose(tp[:, i, u, :], words[:, 2 * b + i, u : D // 2 : 2], ident[:])
            copy(out=gw[:, 2 * b : 2 * b + 2], in_=tp[:].rearrange("p i u r -> p i r u"))

        def quantize_input(side, h, n0=0, n=HALF):
            if n0 == 0:
                cd = keep.tile([P, HALF], U32, name=f"in_codes_{side}{h}", align_bytes=64)
                sc = keep.tile([P, HALF], U8, name=f"in_scales_{side}{h}", align_bytes=64)
                codes[side, h] = (cd, sc)
            cd, sc = codes[side, h]
            nc.vector.quantize_mx(
                out=cd[:, n0 : n0 + n].bitcast(FP8X4), scales=sc[:, n0 : n0 + n],
                in_=grouped_of[side, h][:, n0 : n0 + n].rearrange("p n t -> p (n t)"),
            )

        def widen(h):
            yb = work.tile([P, 4, D], BF16, name="y_bf", align_bytes=64)
            for i in range(4):
                for j in range(4):
                    cols = slice(128 * j, 128 * j + 128)
                    nc.scalar.activation(
                        out=yb[:, i, cols], in_=y_sb[h][:, i, cols].bitcast(FP8), func=ACTF.Copy, scale=ysc[:, 4 * h + i, j : j + 1]
                    )
            return yb

        phasor = {}
        state = {}

        def matmuls(ch):
            side, h, g, n0, n = ch
            cd, sc = codes[side, h]
            banks = []
            for t in range(4):
                ps = psum.tile([P, HALF], F32, name="ps", tag="ps")
                col = slice((4 * g + t) * P, (4 * g + t + 1) * P)
                nc.tensor.matmul_mx(
                    out=ps[:, :n], lhsT=wp[:, col].bitcast(FP8X4), lhsT_scale=wsp[:, col],
                    rhs=cd[:, n0 : n0 + n].bitcast(FP8X4), rhs_scale=sc[:, n0 : n0 + n], start=True, stop=True,
                )
                banks.append(ps)
            state[ch, "banks"] = banks

        def reduce(ch):
            side, h, g, n0, n = ch
            banks = state[ch, "banks"]
            k_sb = work.tile([P, 4, HALF], I32, name="k_sb", align_bytes=64)
            r_sb = work.tile([P, 4, HALF], F32, name="r_sb", align_bytes=64)
            period = PI if KIND[ch] == "P" else 2 * PI

            def count(t):
                if side == "q":
                    off = PI / 4 if KIND[ch] == "P" else -PI / 4
                else:
                    off = (role_k if KIND[ch] == "P" else role_a)[:, g, t : t + 1]
                nc.vector.tensor_scalar(k_sb[:, t, :n], banks[t][:, :n], off, 1.0 / period, op0=ALU.add, op1=ALU.mult)

            def rest(t):
                nc.vector.scalar_tensor_tensor(
                    out=r_sb[:, t, :n], in0=k_sb[:, t, :n], scalar=-period, in1=banks[t][:, :n], op0=ALU.mult, op1=ALU.add
                )

            count(0)
            for t in range(1, 4):
                count(t)
                rest(t - 1)
            rest(3)
            state[ch, "r"] = r_sb
            state[ch, "k"] = k_sb

        def amplitude(ch):
            side, h, g, n0, n = ch
            if KIND[ch] == "P":
                signed = work.tile([P, 4, HALF], I32, name="signed", align_bytes=64)
                nc.vector.scalar_tensor_tensor(
                    out=signed[:, :, :n], in0=state[ch, "k"][:, :, :n], scalar=31,
                    in1=(c32 if side == "k" else a32)[:].bitcast(I32)[:, g, :].unsqueeze(2).to_broadcast([P, 4, n]),
                    op0=ALU.logical_shift_left, op1=ALU.bitwise_xor,
                )
                state[ch, "amp"] = signed[:, :, :n].bitcast(F32).rearrange("p t (c i) -> p c t i", i=4)
            else:
                camp = work.tile([P, 4], F32, name="camp")
                nc.vector.tensor_copy(out=camp[:], in_=vec["a" if side == "q" else "c"][:, g, :])
                state[ch, "amp_v"] = amp_ps[:, "qk".index(side), g, :].unsqueeze(1).unsqueeze(3).to_broadcast([P, n // 4, 4, 4])
                state[ch, "amp"] = camp[:].unsqueeze(1).unsqueeze(3).to_broadcast([P, n // 4, 4, 4])

        def waves(ch):
            side, h, g, n0, n = ch
            r_sb = state[ch, "r"]
            for part in ("im", "re"):
                s_sb = work.tile([P, 4, HALF], F32, name="s_sb", bufs=4, align_bytes=64)
                if KIND[ch] == "P":
                    if side == "q":
                        nc.scalar.activation(out=s_sb[:, :, :n], in_=r_sb[:, :, :n], func=ACTF.Sin, bias=0.0 if part == "im" else half_pi[:])
                    else:
                        for t in range(4):
                            bias = (role_s if part == "im" else role_c)[:, g, t : t + 1]
                            nc.scalar.activation(out=s_sb[:, t, :n], in_=r_sb[:, t, :n], func=ACTF.Sin, bias=bias)
                else:
                    w_sb = work.tile([P, 4, HALF], F32, name="w_sb", align_bytes=64)
                    if side == "q":
                        nc.scalar.activation(out=w_sb[:, :, :n], in_=r_sb[:, :, :n], func=ACTF.Abs, bias=0.0 if part == "re" else neg_half_pi[:])
                    else:
                        for t in range(4):
                            bias = (role_n if part == "im" else role_s)[:, g, t : t + 1]
                            nc.scalar.activation(out=w_sb[:, t, :n], in_=r_sb[:, t, :n], func=ACTF.Abs, bias=bias)
                    nc.scalar.activation(out=s_sb[:, :, :n], in_=w_sb[:, :, :n], func=ACTF.Sin, scale=-1.0, bias=half_pi[:])
                state[ch, part] = s_sb

        def scale(ch, part, eng, lo=0, hi=None):
            n = ch[4]
            hi = n if hi is None else hi
            if (ch, part, "ph") not in state:
                ph = work.tile([P, HALF, 4], BF16, name=f"ph_{part}", align_bytes=64)
                state[ch, part, "ph"] = ph
            ph = state[ch, part, "ph"]
            c0, c1 = lo // 4, hi // 4
            eng.tensor_tensor(
                out=ph[:, :n].rearrange("p (c i) t -> p c t i", i=4)[:, c0:c1],
                in0=state[ch, part][:, :, :n].rearrange("p t (c i) -> p c t i", i=4)[:, c0:c1],
                in1=state[ch, "amp_v" if eng is nc.vector and KIND[ch] == "A" else "amp"][:, c0:c1], op=ALU.mult,
            )

        def quantize(ch, part):
            side, h, g, n0, n = ch
            if (side, h, g, part) not in phasor:
                pc = keep.tile([P, HALF], U32, name=f"pc_{side}{h}{g}{part}", align_bytes=64)
                psc = keep.tile([P, HALF], U8, name=f"psc_{side}{h}{g}{part}", align_bytes=64)
                phasor[side, h, g, part] = (pc, psc)
            pc, psc = phasor[side, h, g, part]
            nc.vector.quantize_mx(
                out=pc[:, n0 : n0 + n].bitcast(FP8X4), scales=psc[:, n0 : n0 + n],
                in_=state[ch, part, "ph"][:, :n].rearrange("p n t -> p (n t)"),
            )

        def passes(dst, qi, kh, g, n0, n, first, last):
            qh, qs = qi // 4, slice(P * (qi % 4), P * (qi % 4) + P)
            for part in ("im", "re"):
                lc, ls = phasor["q", qh, g, part]
                rc, rs = phasor["k", kh, g, part]
                nc.tensor.matmul_mx(
                    out=dst, lhsT=lc[:, qs].bitcast(FP8X4), lhsT_scale=ls[:, qs],
                    rhs=rc[:, n0 : n0 + n].bitcast(FP8X4), rhs_scale=rs[:, n0 : n0 + n],
                    start=first and part == "im", stop=last and part == "re",
                )

        def leave(acc, qi, col, n, eng):
            o_sb = work.tile([P, HALF], F32, name="o_sb", bufs=8, align_bytes=64)
            if eng == "v":
                nc.vector.tensor_scalar(o_sb[:, :n], acc[:, :n], 1.0 / 32.0, None, op0=ALU.mult)
            else:
                nc.scalar.activation(out=o_sb[:, :n], in_=acc[:, :n], func=ACTF.Copy, scale=1.0 / 32.0)
            nc.sync.dma_start(out=out[P * qi : P * qi + P, col : col + n], in_=o_sb[:, :n])

        def product(qi, kh, n0=0, n=HALF, eng="s"):
            acc = psum.tile([P, HALF], F32, name="acc", tag="acc")
            passes(acc[:, :n], qi, kh, 0, n0, n, True, False)
            passes(acc[:, :n], qi, kh, 1, n0, n, False, True)
            leave(acc, qi, HALF * kh + n0, n, eng)

        order = ORDER
        sc, vc = nc.scalar.copy, nc.vector.tensor_copy
        accs = {}

        def start(qi, kh, tag):
            acc = psum.tile([P, HALF], F32, name="acc", tag=tag, bufs=3 if tag == "acc" else 4)
            passes(acc[:], qi, kh, 0, 0, HALF, True, False)
            accs[qi, kh] = acc

        def finish(qi, kh):
            passes(accs[qi, kh][:], qi, kh, 1, 0, HALF, False, True)

        def leave_tile(qi, kh, eng):
            leave(accs[qi, kh], qi, HALF * kh, HALF, eng)

        turn("q", 0, 0, x_sb[0], sc)
        weights(0)
        quantize_input("q", 0, 0, 256)
        matmuls(order[0])
        constants()
        turn("q", 0, 1, x_sb[0], sc)
        yb0 = widen(0)
        LASTN = len(order) - 1
        for n, ch in enumerate(order):
            prev = order[n - 1] if n else None
            reduce(ch)
            if n == 0:
                quantize_input("q", 0, 256, 256)
                weights(1)
                amplitude(ch)
                matmuls(order[1])
                waves(ch)
                turn("k", 0, 0, yb0, sc)
                turn("k", 0, 1, yb0, sc)
                continue
            share, extra = G_SHARE.get(n - 1, (prev[4], 0))
            if share:
                scale(prev, "im", nc.gpsimd, 0, share)
            if extra:
                scale(prev, "re", nc.gpsimd, 0, extra)
            for qi, kh, eng in LEAVES.get(n, []):
                if eng == "v":
                    leave_tile(qi, kh, "v")
            if n == 1:
                quantize_input("k", 0)
            if n == 3:
                turn("k", 1, 0, yb1, sc)
                turn("k", 1, 1, yb1, sc)
            if n == 5:
                turn("q", 1, 0, x_sb[1], sc)
                turn("q", 1, 1, x_sb[1], sc)
            scale(prev, "re", nc.vector, extra, prev[4])
            if share < prev[4]:
                scale(prev, "im", nc.vector, share, prev[4])
                quantize(prev, "re")
                quantize(prev, "im")
            else:
                quantize(prev, "im")
                quantize(prev, "re")
            if n == 3:
                quantize_input("k", 1)
            if n == 5:
                quantize_input("q", 1)
            amplitude(ch)
            if n < LASTN:
                matmuls(order[n + 1])
            for qi, kh, eng in [e for e in LEAVES.get(n, []) if e[2] == "s"] + [e for e in LEAVES.get(n + 1, []) if e[2] == "v"]:
                start(qi, kh, "acc")
                finish(qi, kh)
            waves(ch)

            if n == 1:
                yb1 = widen(1)
            for qi, kh, eng in LEAVES.get(n, []):
                if eng == "s":
                    leave_tile(qi, kh, "s")
        last = order[-1]
        for qi in (6, 7):
            for kh in range(2):
                start(qi, kh, "acc" if (qi, kh) != (7, 1) else "ps")
        for kh in range(2):
            finish(6, kh)
        scale(last, "im", nc.vector)
        scale(last, "re", nc.vector)
        quantize(last, "im")
        quantize(last, "re")
        for kh in range(2):
            leave_tile(6, kh, "vs"[kh])
        for kh in range(2):
            finish(7, kh)
            leave_tile(7, kh, "vs"[kh])
